import numpy as np
import ml_dtypes


def mxq(x, axis, fmt="e4m3"):
    dtype, down = {"e4m3": (ml_dtypes.float8_e4m3fn, 7), "e5m2": (ml_dtypes.float8_e5m2, 14)}[fmt]
    v = np.moveaxis(np.asarray(x, np.float32).astype(ml_dtypes.bfloat16).astype(np.float64), axis, -1)
    blocks = v.reshape(v.shape[:-1] + (-1, 32))
    amax = np.abs(blocks).max(-1, keepdims=True)
    byte = np.maximum(np.where(amax > 0, np.frexp(amax)[1] - 1 + 127, 0) - down, 1)
    scale = np.exp2(byte - 127.0)
    codes = (blocks / scale).astype(np.float32).astype(dtype).astype(np.float64)
    return np.moveaxis((codes * scale).reshape(v.shape), -1, axis)


WIDE = False


def mx_kscale(k):
    if not WIDE:
        return np.ones(k)
    levels = np.array([10, -10, 5, -5, 0])
    if k % 512:
        return np.exp2(np.random.permutation(np.resize(levels, k // 32))).repeat(32)
    a = np.empty((k // 512, 16))
    for p in range(k // 512):
        a[p, :8] = np.random.permutation(np.resize(levels, 8))
        for g in range(8):
            far = levels[np.abs(levels - a[p, g]) >= 10]
            a[p, g + 8] = far[np.random.randint(len(far))]
    return np.exp2(a.ravel()).repeat(32)


BF16 = ml_dtypes.bfloat16


def bf(x):
    return np.asarray(x, np.float32).astype(BF16)


def f64(x):
    return np.asarray(x).astype(np.float64)


E2M1 = np.array([0.0, 0.5, 1.0, 1.5, 2.0, 3.0, 4.0, 6.0, -0.0, -0.5, -1.0, -1.5, -2.0, -3.0, -4.0, -6.0])


def pack_weight(w, fmt):
    k, n = w.shape
    w = f64(bf(w)).reshape(k // 32, 32, n)
    amax = np.abs(w).max(1)
    if fmt == "e4m3":
        byte = np.frexp(amax)[1] - 1 + 127 - 7
    else:
        mant, ex = np.frexp(amax / 6.0)
        byte = np.where(mant > 0.5, ex, ex - 1) + 127
    byte = np.clip(np.where(amax > 0, byte, 1), 1, 254)
    scaled = (w * np.exp2(127.0 - byte)[:, None, :]).reshape(k, n).astype(np.float32)
    by_word = np.ascontiguousarray(scaled.reshape(k // 512, 128, 4, n).transpose(0, 1, 3, 2))
    if fmt == "e4m3":
        words = by_word.astype(ml_dtypes.float8_e4m3fn).view(np.uint8)
    else:
        c = by_word.astype(ml_dtypes.float4_e2m1fn).view(np.uint8) & 0xF
        words = c[..., 0::2] | (c[..., 1::2] << 4)
    return np.ascontiguousarray(words), np.ascontiguousarray(byte.astype(np.uint8).reshape(k // 512, 16, n))


def unpack_weight(words, scales, fmt):
    g, p, n, _ = words.shape
    if fmt == "e4m3":
        vals = np.ascontiguousarray(words).view(ml_dtypes.float8_e4m3fn).astype(np.float64)
    else:
        nib = np.empty((g, p, n, 4), np.uint8)
        nib[..., 0::2] = words & 0xF
        nib[..., 1::2] = words >> 4
        vals = E2M1[nib]
    vals = vals * np.repeat(np.exp2(scales.astype(np.float64) - 127.0), 8, axis=1)[..., None]
    return vals.transpose(0, 1, 3, 2).reshape(g * 512, n)
def pack4(w):
    words, scales = pack_weight(w, "e2m1")
    return words.reshape(words.shape[0], 128, -1), scales


def unpack4(words, scales):
    return unpack_weight(words.reshape(words.shape[0], 128, -1, 2), scales, "e2m1")


G, N = 2, 1024


def setup_inputs():
    s, t = mx_kscale(N), mx_kscale(N)
    a = np.random.standard_normal((G, N, N))
    e = f64(bf((1 + 0.1 * np.random.standard_normal((G, N))) * t))
    u = np.swapaxes(a * e[:, :, None], 1, 2) * s[:, None]
    v = a / e[:, :, None]
    u_words, u_scales = pack4(u.reshape(G * N, N))
    v_words, v_scales = pack4(v.reshape(G * N, N))
    return {"m": bf(3 * np.random.standard_normal((G, N, N)) / N / s[:, None]),
            "u_words": u_words, "u_scales": u_scales,
            "v_words": v_words, "v_scales": v_scales,
            "e": bf(e),
            "step": bf(1 + 0.1 * np.random.standard_normal((G, N)))}


def reference(m, u_words, u_scales, v_words, v_scales, e, step):
    u = unpack4(u_words, u_scales).reshape(G, N, N)
    v = unpack4(v_words, v_scales).reshape(G, N, N)
    am = u.transpose(0, 2, 1) @ mxq(f64(m), 1, "e4m3")
    r = f64(e)[:, :, None] * np.eye(N) - am
    d = v.transpose(0, 2, 1) @ mxq(r, 1, "e4m3")
    return f64(step)[:, None, :] * d

@@ -1,0 +1,267 @@
+from contextlib import ExitStack
+
+import concourse.mybir as mybir
+from concourse.masks import make_identity
+
+G, N = 2, 1024
+FLOPS = 2 * 2 * G * N * N * N
+
+F32 = mybir.dt.float32
+BF16 = mybir.dt.bfloat16
+U32 = mybir.dt.uint32
+I32 = mybir.dt.int32
+U8 = mybir.dt.uint8
+FP8 = mybir.dt.float8_e4m3fn_x4
+FP4 = mybir.dt.float4_e2m1fn_x4
+ALU = mybir.AluOpType
+AX = mybir.AxisListType
+COPY = mybir.ActivationFunctionType.Copy
+
+P = 128
+LAG = 2
+GSET = (3,)
+V_PIECES = ((0, 1), (1, 1), (2, 1), (3, 1))
+
+
+def tile_approximate_inverse_gradient_s14_kernel(tc, m, u_words, u_scales, v_words, v_scales, e, step, out):
+    nc = tc.nc
+    with ExitStack() as ctx:
+        keep = ctx.enter_context(tc.tile_pool(name="keep", bufs=1))
+        mix = ctx.enter_context(tc.tile_pool(name="mix", bufs=4))
+        rpool = ctx.enter_context(tc.tile_pool(name="rpool", bufs=2))
+        opool = ctx.enter_context(tc.tile_pool(name="opool", bufs=8))
+        tpool = ctx.enter_context(tc.tile_pool(name="tpool", bufs=3))
+        ps1p = ctx.enter_context(tc.psum_pool(name="ps1p", bufs=4))
+        ps2p = ctx.enter_context(tc.psum_pool(name="ps2p", bufs=4))
+        ctx.enter_context(tc.manual_schedule())
+
+        u_raw = keep.tile([P, G, 2, 2 * N], U8, name="u_raw", align_bytes=64)
+        u_sraw = keep.tile([P, 2 * G, N], U8, name="u_sraw", align_bytes=64)
+        u_w = keep.tile([P, G, 2, 2, 4, 256], U8, name="u_w", align_bytes=64)
+        u_s = keep.tile([P, G, 2, 2, 4, 128], U8, name="u_s", align_bytes=64)
+        v_raw = keep.tile([P, G, 2, 2 * N], U8, name="v_raw", align_bytes=64)
+        v_s = keep.tile([P, 2 * G, N], U8, name="v_s", align_bytes=64)
+        m_raw = [keep.tile([P, 2, 4, N], BF16, name="m_raw%d" % h, align_bytes=64) for h in range(G)]
+        step_b = keep.tile([P, G * N], BF16, name="step_b", align_bytes=64)
+        e_raw = keep.tile([P, 2 * G, 4], BF16, name="e_raw", align_bytes=64)
+        ident = keep.tile([P, P], BF16, name="ident", align_bytes=64)
+        s4 = keep.tile([P, 32], F32, name="s4", align_bytes=64)
+        qsel = keep.tile([P, 4], F32, name="qsel", align_bytes=64)
+        d4 = keep.tile([P, 2 * G, 16], F32, name="d4", align_bytes=64)
+        ee = keep.tile([P, 2 * G, 128, 4], BF16, name="ee", align_bytes=64)
+
+        u_raw_i = u_raw[:].bitcast(I32)
+        v_raw_i = v_raw[:].bitcast(I32)
+        u_sraw_i = u_sraw[:].bitcast(I32)
+        v_s_i = v_s[:].bitcast(I32)
+        uw_i = u_words.bitcast(I32)
+        vw_i = v_words.bitcast(I32)
+        us_i = u_scales.bitcast(I32)
+        vs_i = v_scales.bitcast(I32)
+
+        nc.vector.memset(u_sraw_i, 0)
+        nc.gpsimd.memset(v_s_i, 0)
+        nc.gpsimd.memset(d4[:], 0.0)
+        make_identity(nc, ident[:])
+
+        def load_u(h, g):
+            nc.sync.dma_start(
+                out=u_raw_i[:, h, :, 256 * g : 256 * g + 256],
+                in_=uw_i[2 * h : 2 * h + 2, :, 256 * g : 256 * g + 256].rearrange("k p n -> p k n"),
+            )
+
+        def load_m(h, k, c0, c1):
+            nc.sync.dma_start(
+                out=m_raw[h][:, k, :, c0:c1],
+                in_=m[h, 512 * k : 512 * k + 512, c0:c1].rearrange("(p t) c -> p t c", t=4),
+            )
+
+        def load_scales(dst, src):
+            for q in range(4):
+                nc.sync.dma_start(
+                    out=dst[32 * q : 32 * q + 4, :, :],
+                    in_=src[:, 4 * q : 4 * q + 4, :].rearrange("k r n -> r k n"),
+                )
+
+        load_u(0, 0)
+        load_m(0, 0, 0, 256)
+        load_m(0, 1, 0, 256)
+        load_scales(u_sraw_i, us_i)
+        load_u(0, 1)
+        nc.sync.dma_start(out=e_raw[:], in_=e.rearrange("h (g p t) -> p (h g) t", g=2, t=4))
+        load_m(0, 0, 256, 512)
+        load_m(0, 1, 256, 512)
+        nc.sync.dma_start(out=v_raw_i[:, 0], in_=vw_i[0:2].rearrange("k p n -> p k n"))
+        load_scales(v_s_i, vs_i)
+        load_m(0, 0, 512, 1024)
+        load_m(0, 1, 512, 1024)
+        nc.sync.dma_start(out=step_b[:], in_=step.rearrange("h c -> (h c)").partition_broadcast(P))
+        load_u(1, 0)
+        load_u(1, 1)
+        load_m(1, 0, 0, 1024)
+        load_m(1, 1, 0, 1024)
+        nc.sync.dma_start(out=v_raw_i[:, 1], in_=vw_i[2:4].rearrange("k p n -> p k n"))
+
+        nc.vector.tensor_reduce(out=s4[:], in_=ident[:].rearrange("p (q r) -> p r q", q=4), axis=AX.X, op=ALU.add)
+        nc.vector.tensor_reduce(out=qsel[:], in_=ident[:].rearrange("p (q r) -> p q r", q=4), axis=AX.X, op=ALU.add)
+
+        def permute_u(eng, h, g):
+            for k in range(2):
+                eng.tensor_copy(
+                    out=u_w[:, h, g, k].rearrange("p t (r b) -> p t r b", b=2),
+                    in_=u_raw[:, h, k, 1024 * g : 1024 * g + 1024].rearrange("p (r t b) -> p t r b", t=4, b=2),
+                )
+            eng.tensor_copy(
+                out=u_s[:, h, g],
+                in_=u_sraw[:, 2 * h : 2 * h + 2, 512 * g : 512 * g + 512].rearrange("p k (r t) -> p k t r", t=4),
+            )
+
+        def build_ee(h):
+            for g in range(2):
+                hg = 2 * h + g
+                nc.gpsimd.tensor_tensor(
+                    out=ee[:, hg].rearrange("p (r a) t -> p r (a t)", a=4),
+                    in0=s4[:].unsqueeze(2).to_broadcast([P, 32, 16]),
+                    in1=d4[:, hg].unsqueeze(1).to_broadcast([P, 32, 16]),
+                    op=ALU.mult,
+                )
+
+        nc.gpsimd.tensor_copy(out=d4[:, :, 0:16:5], in_=e_raw[:])
+        build_ee(0)
+
+        mi = {}
+        mq = {}
+
+        def interleave(cc):
+            h, c0 = cc // 8, 128 * (cc % 8)
+            t = mix.tile([P, 2, 128, 4], BF16, name="mi", align_bytes=64)
+            mi[cc] = t
+            src = m_raw[h][:, :, :, c0 : c0 + 128]
+            if (cc, 1) in V_PIECES:
+                nc.scalar.copy(out=t[:, 0], in_=src[:, 0].rearrange("p t c -> p c t"))
+                nc.vector.tensor_copy(out=t[:, 1], in_=src[:, 1].rearrange("p t c -> p c t"))
+            else:
+                nc.scalar.copy(out=t[:], in_=src.rearrange("p k t c -> p k c t"))
+
+        def quant_m(cc):
+            codes = mix.tile([P, 256], U32, name="mcodes", align_bytes=64)
+            scales = mix.tile([P, 256], U8, name="mscales", align_bytes=64)
+            mq[cc] = (codes, scales)
+            nc.vector.quantize_mx(
+                out=codes[:].bitcast(FP8), scales=scales[:], in_=mi[cc][:].rearrange("p k c t -> p (k c t)")
+            )
+
+        units = {}
+        ps1 = {}
+        ps2 = {}
+
+        def s1_parts(n):
+            unit, i = n // 8, n % 8
+            h, half = unit // 2, unit % 2
+            q = i // 2
+            g = half if i % 2 == 0 else 1 - half
+            return unit, h, half, q, g
+
+        def s1_mm(n):
+            unit, h, half, q, g = s1_parts(n)
+            codes, scales = mq[n // 2]
+            ps = ps1p.tile([P, 4, 128], F32, name="ps1")
+            ps1[n] = ps
+            for t in range(4):
+                for k in range(2):
+                    nc.tensor.matmul_mx(
+                        out=ps[:, t, :],
+                        lhsT=u_w[:, h, g, k, t, :].bitcast(FP4),
+                        lhsT_scale=u_s[:, h, g, k, t, :],
+                        rhs=codes[:, 128 * k : 128 * k + 128].bitcast(FP8),
+                        rhs_scale=scales[:, 128 * k : 128 * k + 128],
+                        start=(k == 0),
+                        stop=(k == 1),
+                    )
+
+        def s1_evac(n):
+            unit, h, half, q, g = s1_parts(n)
+            if n % 8 == 0:
+                units[unit] = (
+                    rpool.tile([P, 2, 512, 4], BF16, name="rb", align_bytes=64),
+                    rpool.tile([P, 2, 512], U32, name="rcodes", align_bytes=64),
+                    rpool.tile([P, 2, 512], U8, name="rscales", align_bytes=64),
+                )
+            rb = units[unit][0]
+            dst = rb[:, g, 128 * q : 128 * q + 128, :]
+            src = ps1[n][:].rearrange("p t c -> p c t")
+            if g == half:
+                nc.vector.scalar_tensor_tensor(
+                    out=dst, in0=ee[:, 2 * h + g], scalar=qsel[:, q : q + 1], in1=src, op0=ALU.mult, op1=ALU.subtract
+                )
+            else:
+                nc.scalar.activation(out=dst, in_=src, func=COPY, scale=-1.0)
+
+        def quant_r(unit, b):
+            rb, rc, rs = units[unit]
+            for g in range(2):
+                cols = slice(256 * b, 256 * b + 256)
+                nc.vector.quantize_mx(
+                    out=rc[:, g, cols].bitcast(FP8),
+                    scales=rs[:, g, cols],
+                    in_=rb[:, g, cols, :].rearrange("p c t -> p (c t)"),
+                )
+
+        def s2_mm(n):
+            unit, j = n // 8, n % 8
+            h = unit // 2
+            rb, rc, rs = units[unit]
+            ps = ps2p.tile([P, 512], F32, name="ps2")
+            ps2[n] = ps
+            for g in range(2):
+                nc.tensor.matmul_mx(
+                    out=ps[:],
+                    lhsT=v_raw[:, h, g, 256 * j : 256 * j + 256].bitcast(FP4),
+                    lhsT_scale=v_s[:, 2 * h + g, 128 * j : 128 * j + 128],
+                    rhs=rc[:, g, :].bitcast(FP8),
+                    rhs_scale=rs[:, g, :],
+                    start=(g == 0),
+                    stop=(g == 1),
+                )
+
+        def s2_evac(n):
+            unit, j = n // 8, n % 8
+            h, c0 = unit // 2, 512 * (unit % 2)
+            ot = opool.tile([P, 512], F32, name="ot", align_bytes=64)
+            st = step_b[:, N * h + c0 : N * h + c0 + 512]
+            if j in GSET:
+                tmp = tpool.tile([P, 512], F32, name="tmp", align_bytes=64)
+                nc.scalar.copy(out=tmp[:], in_=ps2[n][:])
+                nc.gpsimd.tensor_tensor(out=ot[:], in0=tmp[:], in1=st, op=ALU.mult)
+            else:
+                nc.vector.tensor_tensor(out=ot[:], in0=ps2[n][:], in1=st, op=ALU.mult)
+            nc.sync.dma_start(out=out[h, 128 * j : 128 * j + 128, c0 : c0 + 512], in_=ot[:])
+
+        interleave(0)
+        permute_u(nc.vector, 0, 0)
+        quant_m(0)
+        interleave(1)
+        permute_u(nc.vector, 0, 1)
+        build_ee(1)
+        permute_u(nc.gpsimd, 1, 0)
+        permute_u(nc.gpsimd, 1, 1)
+
+        S = 32
+        for n in range(S + 8 + LAG + 1):
+            if n % 2 == 0:
+                cc = n // 2
+                if cc + 2 < 16:
+                    interleave(cc + 2)
+                if cc + 1 < 16:
+                    quant_m(cc + 1)
+            if n < S:
+                s1_mm(n)
+            k = n - 8 - LAG
+            if 0 <= k < S:
+                s2_mm(k)
+            if 0 <= n - 1 < S:
+                s1_evac(n - 1)
+            if 0 <= k - 1 < S:
+                s2_evac(k - 1)
+            if 1 <= n <= S and (n - 1) % 4 == 3:
+                quant_r((n - 1) // 8, ((n - 1) % 8) // 4)

@@ -19,7 +19,7 @@ COPY = mybir.ActivationFunctionType.Copy
 
 P = 128
 LAG = 2
-GSET = (3,)
+GSET = (1, 4, 6)
 V_PIECES = ((0, 1), (1, 1), (2, 1), (3, 1))
 
 
@@ -47,7 +47,6 @@ def tile_approximate_inverse_gradient_s14_kernel(tc, m, u_words, u_scales, v_wor
         ident = keep.tile([P, P], BF16, name="ident", align_bytes=64)
         s4 = keep.tile([P, 32], F32, name="s4", align_bytes=64)
         qsel = keep.tile([P, 4], F32, name="qsel", align_bytes=64)
-        d4 = keep.tile([P, 2 * G, 16], F32, name="d4", align_bytes=64)
         ee = keep.tile([P, 2 * G, 128, 4], BF16, name="ee", align_bytes=64)
 
         u_raw_i = u_raw[:].bitcast(I32)
@@ -61,7 +60,7 @@ def tile_approximate_inverse_gradient_s14_kernel(tc, m, u_words, u_scales, v_wor
 
         nc.vector.memset(u_sraw_i, 0)
         nc.gpsimd.memset(v_s_i, 0)
-        nc.gpsimd.memset(d4[:], 0.0)
+        nc.gpsimd.memset(ee[:].rearrange("p a b c -> p (a b c)").bitcast(I32), 0)
         make_identity(nc, ident[:])
 
         def load_u(h, g):
@@ -76,28 +75,31 @@ def tile_approximate_inverse_gradient_s14_kernel(tc, m, u_words, u_scales, v_wor
                 in_=m[h, 512 * k : 512 * k + 512, c0:c1].rearrange("(p t) c -> p t c", t=4),
             )
 
-        def load_scales(dst, src):
+        def load_scales(dst, src, a, b):
             for q in range(4):
                 nc.sync.dma_start(
-                    out=dst[32 * q : 32 * q + 4, :, :],
-                    in_=src[:, 4 * q : 4 * q + 4, :].rearrange("k r n -> r k n"),
+                    out=dst[32 * q : 32 * q + 4, a:b, :],
+                    in_=src[a:b, 4 * q : 4 * q + 4, :].rearrange("k r n -> r k n"),
                 )
 
         load_u(0, 0)
-        load_m(0, 0, 0, 256)
-        load_m(0, 1, 0, 256)
-        load_scales(u_sraw_i, us_i)
+        load_m(0, 0, 0, 128)
+        load_m(0, 1, 0, 128)
+        load_scales(u_sraw_i, us_i, 0, 2)
+        load_m(0, 0, 128, 256)
+        load_m(0, 1, 128, 256)
         load_u(0, 1)
         nc.sync.dma_start(out=e_raw[:], in_=e.rearrange("h (g p t) -> p (h g) t", g=2, t=4))
         load_m(0, 0, 256, 512)
         load_m(0, 1, 256, 512)
-        nc.sync.dma_start(out=v_raw_i[:, 0], in_=vw_i[0:2].rearrange("k p n -> p k n"))
-        load_scales(v_s_i, vs_i)
         load_m(0, 0, 512, 1024)
         load_m(0, 1, 512, 1024)
-        nc.sync.dma_start(out=step_b[:], in_=step.rearrange("h c -> (h c)").partition_broadcast(P))
         load_u(1, 0)
         load_u(1, 1)
+        load_scales(u_sraw_i, us_i, 2, 4)
+        nc.sync.dma_start(out=v_raw_i[:, 0], in_=vw_i[0:2].rearrange("k p n -> p k n"))
+        load_scales(v_s_i, vs_i, 0, 4)
+        nc.sync.dma_start(out=step_b[:], in_=step.rearrange("h c -> (h c)").partition_broadcast(P))
         load_m(1, 0, 0, 1024)
         load_m(1, 1, 0, 1024)
         nc.sync.dma_start(out=v_raw_i[:, 1], in_=vw_i[2:4].rearrange("k p n -> p k n"))
@@ -105,13 +107,14 @@ def tile_approximate_inverse_gradient_s14_kernel(tc, m, u_words, u_scales, v_wor
         nc.vector.tensor_reduce(out=s4[:], in_=ident[:].rearrange("p (q r) -> p r q", q=4), axis=AX.X, op=ALU.add)
         nc.vector.tensor_reduce(out=qsel[:], in_=ident[:].rearrange("p (q r) -> p q r", q=4), axis=AX.X, op=ALU.add)
 
-        def permute_u(eng, h, g):
-            for k in range(2):
-                eng.tensor_copy(
-                    out=u_w[:, h, g, k].rearrange("p t (r b) -> p t r b", b=2),
-                    in_=u_raw[:, h, k, 1024 * g : 1024 * g + 1024].rearrange("p (r t b) -> p t r b", t=4, b=2),
-                )
-            eng.tensor_copy(
+        def permute_codes(h, g, k):
+            nc.vector.tensor_copy(
+                out=u_w[:, h, g, k].rearrange("p t (r b) -> p t r b", b=2),
+                in_=u_raw[:, h, k, 1024 * g : 1024 * g + 1024].rearrange("p (r t b) -> p t r b", t=4, b=2),
+            )
+
+        def permute_scales(h, g):
+            nc.vector.tensor_copy(
                 out=u_s[:, h, g],
                 in_=u_sraw[:, 2 * h : 2 * h + 2, 512 * g : 512 * g + 512].rearrange("p k (r t) -> p k t r", t=4),
             )
@@ -119,15 +122,12 @@ def tile_approximate_inverse_gradient_s14_kernel(tc, m, u_words, u_scales, v_wor
         def build_ee(h):
             for g in range(2):
                 hg = 2 * h + g
-                nc.gpsimd.tensor_tensor(
-                    out=ee[:, hg].rearrange("p (r a) t -> p r (a t)", a=4),
-                    in0=s4[:].unsqueeze(2).to_broadcast([P, 32, 16]),
-                    in1=d4[:, hg].unsqueeze(1).to_broadcast([P, 32, 16]),
+                nc.vector.tensor_tensor(
+                    out=ee[:, hg].rearrange("p x t -> p (x t)").rearrange("p (r a) -> p r a", a=16)[:, :, 0:16:5],
+                    in0=s4[:].unsqueeze(2).to_broadcast([P, 32, 4]),
+                    in1=e_raw[:, hg].unsqueeze(1).to_broadcast([P, 32, 4]),
                     op=ALU.mult,
                 )
-
-        nc.gpsimd.tensor_copy(out=d4[:, :, 0:16:5], in_=e_raw[:])
-        build_ee(0)
 
         mi = {}
         mq = {}
@@ -232,19 +232,24 @@ def tile_approximate_inverse_gradient_s14_kernel(tc, m, u_words, u_scales, v_wor
             if j in GSET:
                 tmp = tpool.tile([P, 512], F32, name="tmp", align_bytes=64)
                 nc.scalar.copy(out=tmp[:], in_=ps2[n][:])
-                nc.gpsimd.tensor_tensor(out=ot[:], in0=tmp[:], in1=st, op=ALU.mult)
+                for a in (0, 256):
+                    nc.gpsimd.tensor_tensor(
+                        out=ot[:, a : a + 256], in0=tmp[:, a : a + 256], in1=st[:, a : a + 256], op=ALU.mult
+                    )
             else:
                 nc.vector.tensor_tensor(out=ot[:], in0=ps2[n][:], in1=st, op=ALU.mult)
             nc.sync.dma_start(out=out[h, 128 * j : 128 * j + 128, c0 : c0 + 512], in_=ot[:])
 
         interleave(0)
-        permute_u(nc.vector, 0, 0)
+        permute_codes(0, 0, 0)
+        permute_codes(0, 0, 1)
+        permute_scales(0, 0)
         quant_m(0)
         interleave(1)
-        permute_u(nc.vector, 0, 1)
-        build_ee(1)
-        permute_u(nc.gpsimd, 1, 0)
-        permute_u(nc.gpsimd, 1, 1)
+        permute_codes(0, 1, 0)
+        permute_codes(0, 1, 1)
+        permute_scales(0, 1)
+        build_ee(0)
 
         S = 32
         for n in range(S + 8 + LAG + 1):
@@ -263,5 +268,13 @@ def tile_approximate_inverse_gradient_s14_kernel(tc, m, u_words, u_scales, v_wor
                 s1_evac(n - 1)
             if 0 <= k - 1 < S:
                 s2_evac(k - 1)
+            if n == 2:
+                build_ee(1)
+            if 3 <= n < 15 and n % 2 == 1:
+                g, piece = (n - 3) // 6, (n - 3) // 2 % 3
+                if piece < 2:
+                    permute_codes(1, g, piece)
+                else:
+                    permute_scales(1, g)
             if 1 <= n <= S and (n - 1) % 4 == 3:
                 quant_r((n - 1) // 8, ((n - 1) % 8) // 4)

@@ -18,9 +18,7 @@ AX = mybir.AxisListType
 COPY = mybir.ActivationFunctionType.Copy
 
 P = 128
-LAG = 2
-GSET = (1, 4, 6)
-V_PIECES = ((0, 1), (1, 1), (2, 1), (3, 1))
+CFG = dict(list(({'lag': 3, 'gset': {0: (1, 3, 5), 1: (), 2: (), 3: ()}, 'vp': ((0, 1), (1, 1), (2, 1), (3, 1)), 'look': 2, 'ql': 1, 'd1': 1, 'd2': 1, 'perm': (7, 8, 9, 10, 11, 12), 'rq': 1, 'ee1': 8, 'spread': 3, 'p01': 1, 'order': 3, 'halves': 1, 'c128': 0, 'ord0': ((0, 0), (1, 0), (0, 1), (1, 1), (2, 0), (3, 0), (2, 1), (3, 1)), 'ordn': ((0, 0), (0, 1), (1, 0), (1, 1), (2, 0), (2, 1), (3, 0), (3, 1)), 'ia': 4, 'qa': 3, 'sd': 2, 'u01': 1, 'mem': 0}).items()) + list(dict(p01=2,u01=0,c128=1).items()))
 
 
 def tile_approximate_inverse_gradient_s14_kernel(tc, m, u_words, u_scales, v_words, v_scales, e, step, out):
@@ -43,6 +41,8 @@ def tile_approximate_inverse_gradient_s14_kernel(tc, m, u_words, u_scales, v_wor
         v_s = keep.tile([P, 2 * G, N], U8, name="v_s", align_bytes=64)
         m_raw = [keep.tile([P, 2, 4, N], BF16, name="m_raw%d" % h, align_bytes=64) for h in range(G)]
         step_b = keep.tile([P, G * N], BF16, name="step_b", align_bytes=64)
+        srow = keep.tile([P, P], BF16, name="srow", align_bytes=64)
+        scol = keep.tile([P, 16], BF16, name="scol", align_bytes=64)
         e_raw = keep.tile([P, 2 * G, 4], BF16, name="e_raw", align_bytes=64)
         ident = keep.tile([P, P], BF16, name="ident", align_bytes=64)
         s4 = keep.tile([P, 32], F32, name="s4", align_bytes=64)
@@ -59,9 +59,10 @@ def tile_approximate_inverse_gradient_s14_kernel(tc, m, u_words, u_scales, v_wor
         vs_i = v_scales.bitcast(I32)
 
         nc.vector.memset(u_sraw_i, 0)
+        nc.gpsimd.memset(srow[:].bitcast(I32), 0)
+        make_identity(nc, ident[:])
         nc.gpsimd.memset(v_s_i, 0)
         nc.gpsimd.memset(ee[:].rearrange("p a b c -> p (a b c)").bitcast(I32), 0)
-        make_identity(nc, ident[:])
 
         def load_u(h, g):
             nc.sync.dma_start(
@@ -82,27 +83,56 @@ def tile_approximate_inverse_gradient_s14_kernel(tc, m, u_words, u_scales, v_wor
                     in_=src[a:b, 4 * q : 4 * q + 4, :].rearrange("k r n -> r k n"),
                 )
 
+        def load_small():
+            nc.sync.dma_start(out=srow[0:16, :], in_=step.rearrange("h (a n) -> (h a) n", n=P))
+            nc.sync.dma_start(out=e_raw[:], in_=e.rearrange("h (g p t) -> p (h g) t", g=2, t=4))
+
+        def load_v(h):
+            nc.sync.dma_start(out=v_raw_i[:, h], in_=vw_i[2 * h : 2 * h + 2].rearrange("k p n -> p k n"))
+
         load_u(0, 0)
-        load_m(0, 0, 0, 128)
-        load_m(0, 1, 0, 128)
-        load_scales(u_sraw_i, us_i, 0, 2)
-        load_m(0, 0, 128, 256)
-        load_m(0, 1, 128, 256)
-        load_u(0, 1)
-        nc.sync.dma_start(out=e_raw[:], in_=e.rearrange("h (g p t) -> p (h g) t", g=2, t=4))
-        load_m(0, 0, 256, 512)
-        load_m(0, 1, 256, 512)
-        load_m(0, 0, 512, 1024)
-        load_m(0, 1, 512, 1024)
-        load_u(1, 0)
-        load_u(1, 1)
-        load_scales(u_sraw_i, us_i, 2, 4)
-        nc.sync.dma_start(out=v_raw_i[:, 0], in_=vw_i[0:2].rearrange("k p n -> p k n"))
-        load_scales(v_s_i, vs_i, 0, 4)
-        nc.sync.dma_start(out=step_b[:], in_=step.rearrange("h c -> (h c)").partition_broadcast(P))
-        load_m(1, 0, 0, 1024)
-        load_m(1, 1, 0, 1024)
-        nc.sync.dma_start(out=v_raw_i[:, 1], in_=vw_i[2:4].rearrange("k p n -> p k n"))
+        if CFG["mem"] == 0:
+            load_scales(u_sraw_i, us_i, 0, 2)
+        if CFG["u01"] == 1:
+            load_u(0, 1)
+        first = (0, 128, 256) if CFG["c128"] else (0, 256)
+        for i, (a, b) in enumerate(zip(first[:-1], first[1:])):
+            load_m(0, 0, a, b)
+            load_m(0, 1, a, b)
+            if i == 0:
+                if CFG["mem"] == 1:
+                    load_scales(u_sraw_i, us_i, 0, 2)
+                if CFG["u01"] == 0:
+                    load_u(0, 1)
+        if CFG["u01"] == 2:
+            load_u(0, 1)
+        load_small()
+        if CFG["order"] % 2:
+            load_m(0, 0, 256, 1024)
+            load_m(0, 1, 256, 1024)
+        else:
+            load_m(0, 0, 256, 512)
+            load_m(0, 1, 256, 512)
+            load_m(0, 0, 512, 1024)
+            load_m(0, 1, 512, 1024)
+        load_v(0)
+        load_scales(v_s_i, vs_i, 0, 2)
+        if CFG["order"] // 2 == 0:
+            load_u(1, 0)
+            load_u(1, 1)
+            load_scales(u_sraw_i, us_i, 2, 4)
+            load_m(1, 0, 0, 1024)
+            load_m(1, 1, 0, 1024)
+        else:
+            load_u(1, 0)
+            load_m(1, 0, 0, 512)
+            load_m(1, 1, 0, 512)
+            load_u(1, 1)
+            load_scales(u_sraw_i, us_i, 2, 4)
+            load_m(1, 0, 512, 1024)
+            load_m(1, 1, 512, 1024)
+        load_v(1)
+        load_scales(v_s_i, vs_i, 2, 4)
 
         nc.vector.tensor_reduce(out=s4[:], in_=ident[:].rearrange("p (q r) -> p r q", q=4), axis=AX.X, op=ALU.add)
         nc.vector.tensor_reduce(out=qsel[:], in_=ident[:].rearrange("p (q r) -> p q r", q=4), axis=AX.X, op=ALU.add)
@@ -137,9 +167,12 @@ def tile_approximate_inverse_gradient_s14_kernel(tc, m, u_words, u_scales, v_wor
             t = mix.tile([P, 2, 128, 4], BF16, name="mi", align_bytes=64)
             mi[cc] = t
             src = m_raw[h][:, :, :, c0 : c0 + 128]
-            if (cc, 1) in V_PIECES:
-                nc.scalar.copy(out=t[:, 0], in_=src[:, 0].rearrange("p t c -> p c t"))
-                nc.vector.tensor_copy(out=t[:, 1], in_=src[:, 1].rearrange("p t c -> p c t"))
+            for k in range(2):
+                if (cc, k) in CFG["vp"]:
+                    nc.vector.tensor_copy(out=t[:, k], in_=src[:, k].rearrange("p t c -> p c t"))
+            if (cc, 1) in CFG["vp"]:
+                if (cc, 0) not in CFG["vp"]:
+                    nc.scalar.copy(out=t[:, 0], in_=src[:, 0].rearrange("p t c -> p c t"))
             else:
                 nc.scalar.copy(out=t[:], in_=src.rearrange("p k t c -> p k c t"))
 
@@ -151,20 +184,29 @@ def tile_approximate_inverse_gradient_s14_kernel(tc, m, u_words, u_scales, v_wor
                 out=codes[:].bitcast(FP8), scales=scales[:], in_=mi[cc][:].rearrange("p k c t -> p (k c t)")
             )
 
+        order1 = []
+        for unit in range(4):
+            for q, d in CFG["ordn"] if unit else CFG["ord0"]:
+                order1.append((unit, q, d))
+        first_use = {}
+        for i in range(32):
+            first_use.setdefault(4 * order1[i][0] + order1[i][1], i)
+
         units = {}
         ps1 = {}
         ps2 = {}
 
         def s1_parts(n):
-            unit, i = n // 8, n % 8
+            unit, q, d = order1[n]
             h, half = unit // 2, unit % 2
-            q = i // 2
-            g = half if i % 2 == 0 else 1 - half
+            g = half if d == 0 else 1 - half
+            if unit == 0:
+                g = d
             return unit, h, half, q, g
 
         def s1_mm(n):
             unit, h, half, q, g = s1_parts(n)
-            codes, scales = mq[n // 2]
+            codes, scales = mq[4 * order1[n][0] + order1[n][1]]
             ps = ps1p.tile([P, 4, 128], F32, name="ps1")
             ps1[n] = ps
             for t in range(4):
@@ -197,10 +239,11 @@ def tile_approximate_inverse_gradient_s14_kernel(tc, m, u_words, u_scales, v_wor
             else:
                 nc.scalar.activation(out=dst, in_=src, func=COPY, scale=-1.0)
 
-        def quant_r(unit, b):
+        def quant_r(unit, g, b):
             rb, rc, rs = units[unit]
-            for g in range(2):
-                cols = slice(256 * b, 256 * b + 256)
+            if True:
+                w = 512 // CFG["rq"]
+                cols = slice(w * b, w * b + w)
                 nc.vector.quantize_mx(
                     out=rc[:, g, cols].bitcast(FP8),
                     scales=rs[:, g, cols],
@@ -229,52 +272,99 @@ def tile_approximate_inverse_gradient_s14_kernel(tc, m, u_words, u_scales, v_wor
             h, c0 = unit // 2, 512 * (unit % 2)
             ot = opool.tile([P, 512], F32, name="ot", align_bytes=64)
             st = step_b[:, N * h + c0 : N * h + c0 + 512]
-            if j in GSET:
+            if j in CFG["gset"][unit]:
                 tmp = tpool.tile([P, 512], F32, name="tmp", align_bytes=64)
                 nc.scalar.copy(out=tmp[:], in_=ps2[n][:])
-                for a in (0, 256):
-                    nc.gpsimd.tensor_tensor(
-                        out=ot[:, a : a + 256], in0=tmp[:, a : a + 256], in1=st[:, a : a + 256], op=ALU.mult
-                    )
+                w = 512 // CFG["halves"]
+                for a in range(0, 512, w):
+                    nc.gpsimd.tensor_tensor(out=ot[:, a : a + w], in0=tmp[:, a : a + w], in1=st[:, a : a + w], op=ALU.mult)
             else:
                 nc.vector.tensor_tensor(out=ot[:], in0=ps2[n][:], in1=st, op=ALU.mult)
-            nc.sync.dma_start(out=out[h, 128 * j : 128 * j + 128, c0 : c0 + 512], in_=ot[:])
+            stores.append((n + (CFG["sd"] if j in CFG["gset"][unit] else 0), out[h, 128 * j : 128 * j + 128, c0 : c0 + 512], ot))
 
-        interleave(0)
+        stores = []
+
+        def flush(n):
+            for item in list(stores):
+                if item[0] <= n:
+                    nc.sync.dma_start(out=item[1], in_=item[2][:])
+                    stores.remove(item)
+
+        done_i, done_q = set(), set()
+
+        def prepare(n):
+            for cc in range(16):
+                if first_use[cc] <= n + CFG["ia"] and cc not in done_i:
+                    done_i.add(cc)
+                    interleave(cc)
+                if first_use[cc] <= n + CFG["qa"] and cc not in done_q:
+                    done_q.add(cc)
+                    quant_m(cc)
+
         permute_codes(0, 0, 0)
         permute_codes(0, 0, 1)
         permute_scales(0, 0)
+        if CFG["p01"] == 1:
+            permute_codes(0, 1, 0)
+            permute_codes(0, 1, 1)
+            permute_scales(0, 1)
+        interleave(0)
+        done_i.add(0)
         quant_m(0)
-        interleave(1)
-        permute_codes(0, 1, 0)
-        permute_codes(0, 1, 1)
-        permute_scales(0, 1)
+        done_q.add(0)
+        if CFG["p01"] == 2:
+            interleave(1)
+            quant_m(1)
+            done_i.add(1)
+            done_q.add(1)
+        if CFG["p01"] != 1:
+            permute_codes(0, 1, 0)
+            permute_codes(0, 1, 1)
+            permute_scales(0, 1)
         build_ee(0)
 
+        def spread_step():
+            pst = ps2p.tile([P, 1024], BF16, name="ps2")
+            nc.tensor.transpose(pst[:, 0:P], srow[:], ident[:])
+            nc.scalar.copy(out=scol[:], in_=pst[:, 0:16])
+            for h in range(G):
+                psb = ps2p.tile([P, 1024], BF16, name="ps2")
+                for a in range(8):
+                    nc.tensor.transpose(
+                        psb[:, P * a : P * a + P], scol[:, 8 * h + a : 8 * h + a + 1].to_broadcast([P, P]), ident[:]
+                    )
+                nc.scalar.copy(out=step_b[:, N * h : N * h + N], in_=psb[:])
+
         S = 32
-        for n in range(S + 8 + LAG + 1):
-            if n % 2 == 0:
-                cc = n // 2
-                if cc + 2 < 16:
-                    interleave(cc + 2)
-                if cc + 1 < 16:
-                    quant_m(cc + 1)
+        LAG, D1, D2, RQ = CFG["lag"], CFG["d1"], CFG["d2"], CFG["rq"]
+        seen = {}
+        for n in range(S + 8 + LAG + 2):
+            prepare(n)
             if n < S:
                 s1_mm(n)
             k = n - 8 - LAG
             if 0 <= k < S:
                 s2_mm(k)
-            if 0 <= n - 1 < S:
-                s1_evac(n - 1)
-            if 0 <= k - 1 < S:
-                s2_evac(k - 1)
-            if n == 2:
+            a = n - D1
+            if 0 <= a < S:
+                s1_evac(a)
+            if 0 <= k - D2 < S:
+                s2_evac(k - D2)
+            flush(k - D2)
+            if n == CFG["ee1"]:
                 build_ee(1)
-            if 3 <= n < 15 and n % 2 == 1:
-                g, piece = (n - 3) // 6, (n - 3) // 2 % 3
-                if piece < 2:
-                    permute_codes(1, g, piece)
-                else:
-                    permute_scales(1, g)
-            if 1 <= n <= S and (n - 1) % 4 == 3:
-                quant_r((n - 1) // 8, ((n - 1) % 8) // 4)
+            if n == CFG["spread"]:
+                spread_step()
+            for piece in range(6):
+                if CFG["perm"][piece] == n:
+                    if piece % 3 < 2:
+                        permute_codes(1, piece // 3, piece % 3)
+                    else:
+                        permute_scales(1, piece // 3)
+            if 0 <= a < S:
+                unit, h, half, q, g = s1_parts(a)
+                b = q * RQ // 4
+                seen[(unit, g, b)] = seen.get((unit, g, b), 0) + 1
+                if seen[(unit, g, b)] == 4 // RQ:
+                    quant_r(unit, g, b)
+        flush(S + 10)

@@ -18,7 +18,7 @@ AX = mybir.AxisListType
 COPY = mybir.ActivationFunctionType.Copy
 
 P = 128
-CFG = dict(list(({'lag': 3, 'gset': {0: (1, 3, 5), 1: (), 2: (), 3: ()}, 'vp': ((0, 1), (1, 1), (2, 1), (3, 1)), 'look': 2, 'ql': 1, 'd1': 1, 'd2': 1, 'perm': (7, 8, 9, 10, 11, 12), 'rq': 1, 'ee1': 8, 'spread': 3, 'p01': 1, 'order': 3, 'halves': 1, 'c128': 0, 'ord0': ((0, 0), (1, 0), (0, 1), (1, 1), (2, 0), (3, 0), (2, 1), (3, 1)), 'ordn': ((0, 0), (0, 1), (1, 0), (1, 1), (2, 0), (2, 1), (3, 0), (3, 1)), 'ia': 4, 'qa': 3, 'sd': 2, 'u01': 1, 'mem': 0}).items()) + list(dict(p01=2,u01=0,c128=1).items()))
+CFG = {'lag': 2, 'gset': {0: (0, 2, 4), 1: (), 2: (), 3: ()}, 'vp': ((0, 1), (1, 1), (2, 1), (3, 1), (4, 1), (5, 1)), 'd1': 0, 'd2': 0, 'rq': 2, 'ee1': 4, 'spread': 4, 'halves': 2, 'ord0': ((0, 0), (1, 0), (0, 1), (1, 1), (2, 0), (3, 0), (2, 1), (3, 1)), 'ordn': ((0, 0), (0, 1), (1, 0), (1, 1), (2, 0), (2, 1), (3, 0), (3, 1)), 'ia': 3, 'qa': 3, 'sd': 3, 'loads': 'u00 mA us0 mB u01 sm mC mD u10 us1 v0 vs0 u11 n0 n1 vs1 v1', 'g0': '1s 11', 'va': '00 01 0s', 'vb': '10', 'g1': '00 01 10 11 1s', 'v1': ((9, '0s'),), 'first': 2, 'gp': 4}
 
 
 def tile_approximate_inverse_gradient_s14_kernel(tc, m, u_words, u_scales, v_words, v_scales, e, step, out):
@@ -58,10 +58,11 @@ def tile_approximate_inverse_gradient_s14_kernel(tc, m, u_words, u_scales, v_wor
         us_i = u_scales.bitcast(I32)
         vs_i = v_scales.bitcast(I32)
 
-        nc.vector.memset(u_sraw_i, 0)
+        nc.vector.memset(u_sraw_i[:, 0:2], 0)
+        nc.vector.memset(u_sraw_i[:, 2:4], 0)
+        nc.vector.memset(v_s_i, 0)
         nc.gpsimd.memset(srow[:].bitcast(I32), 0)
         make_identity(nc, ident[:])
-        nc.gpsimd.memset(v_s_i, 0)
         nc.gpsimd.memset(ee[:].rearrange("p a b c -> p (a b c)").bitcast(I32), 0)
 
         def load_u(h, g):
@@ -90,64 +91,42 @@ def tile_approximate_inverse_gradient_s14_kernel(tc, m, u_words, u_scales, v_wor
         def load_v(h):
             nc.sync.dma_start(out=v_raw_i[:, h], in_=vw_i[2 * h : 2 * h + 2].rearrange("k p n -> p k n"))
 
-        load_u(0, 0)
-        if CFG["mem"] == 0:
-            load_scales(u_sraw_i, us_i, 0, 2)
-        if CFG["u01"] == 1:
-            load_u(0, 1)
-        first = (0, 128, 256) if CFG["c128"] else (0, 256)
-        for i, (a, b) in enumerate(zip(first[:-1], first[1:])):
-            load_m(0, 0, a, b)
-            load_m(0, 1, a, b)
-            if i == 0:
-                if CFG["mem"] == 1:
-                    load_scales(u_sraw_i, us_i, 0, 2)
-                if CFG["u01"] == 0:
-                    load_u(0, 1)
-        if CFG["u01"] == 2:
-            load_u(0, 1)
-        load_small()
-        if CFG["order"] % 2:
-            load_m(0, 0, 256, 1024)
-            load_m(0, 1, 256, 1024)
-        else:
-            load_m(0, 0, 256, 512)
-            load_m(0, 1, 256, 512)
-            load_m(0, 0, 512, 1024)
-            load_m(0, 1, 512, 1024)
-        load_v(0)
-        load_scales(v_s_i, vs_i, 0, 2)
-        if CFG["order"] // 2 == 0:
-            load_u(1, 0)
-            load_u(1, 1)
-            load_scales(u_sraw_i, us_i, 2, 4)
-            load_m(1, 0, 0, 1024)
-            load_m(1, 1, 0, 1024)
-        else:
-            load_u(1, 0)
-            load_m(1, 0, 0, 512)
-            load_m(1, 1, 0, 512)
-            load_u(1, 1)
-            load_scales(u_sraw_i, us_i, 2, 4)
-            load_m(1, 0, 512, 1024)
-            load_m(1, 1, 512, 1024)
-        load_v(1)
-        load_scales(v_s_i, vs_i, 2, 4)
+        def load_m2(h, a, b):
+            load_m(h, 0, a, b)
+            load_m(h, 1, a, b)
+
+        loads = {
+            "u00": lambda: load_u(0, 0), "u01": lambda: load_u(0, 1), "u10": lambda: load_u(1, 0), "u11": lambda: load_u(1, 1),
+            "us0": lambda: load_scales(u_sraw_i, us_i, 0, 2), "us1": lambda: load_scales(u_sraw_i, us_i, 2, 4),
+            "vs0": lambda: load_scales(v_s_i, vs_i, 0, 2), "vs1": lambda: load_scales(v_s_i, vs_i, 2, 4),
+            "us": lambda: load_scales(u_sraw_i, us_i, 0, 4), "vs": lambda: load_scales(v_s_i, vs_i, 0, 4),
+            "v0": lambda: load_v(0), "v1": lambda: load_v(1), "sm": load_small,
+            "mA": lambda: load_m2(0, 0, 128), "mB": lambda: load_m2(0, 128, 256), "mAB": lambda: load_m2(0, 0, 256),
+            "mC": lambda: load_m2(0, 256, 512), "mD": lambda: load_m2(0, 512, 1024), "mCD": lambda: load_m2(0, 256, 1024),
+            "n0": lambda: load_m2(1, 0, 512), "n1": lambda: load_m2(1, 512, 1024), "n": lambda: load_m2(1, 0, 1024),
+        }
+        for token in CFG["loads"].split():
+            loads[token]()
 
         nc.vector.tensor_reduce(out=s4[:], in_=ident[:].rearrange("p (q r) -> p r q", q=4), axis=AX.X, op=ALU.add)
         nc.vector.tensor_reduce(out=qsel[:], in_=ident[:].rearrange("p (q r) -> p q r", q=4), axis=AX.X, op=ALU.add)
 
-        def permute_codes(h, g, k):
-            nc.vector.tensor_copy(
-                out=u_w[:, h, g, k].rearrange("p t (r b) -> p t r b", b=2),
-                in_=u_raw[:, h, k, 1024 * g : 1024 * g + 1024].rearrange("p (r t b) -> p t r b", t=4, b=2),
-            )
+        def permute_codes(h, g, k, eng, parts):
+            dst = u_w[:, h, g, k].rearrange("p t (r b) -> p t r b", b=2)
+            src = u_raw[:, h, k, 1024 * g : 1024 * g + 1024].rearrange("p (r t b) -> p t r b", t=4, b=2)
+            w = 4 // parts
+            for t in range(0, 4, w):
+                eng.tensor_copy(out=dst[:, t : t + w], in_=src[:, t : t + w])
 
-        def permute_scales(h, g):
-            nc.vector.tensor_copy(
-                out=u_s[:, h, g],
-                in_=u_sraw[:, 2 * h : 2 * h + 2, 512 * g : 512 * g + 512].rearrange("p k (r t) -> p k t r", t=4),
-            )
+        def permute_scales(h, g, eng, parts):
+            src = u_sraw[:, 2 * h : 2 * h + 2, 512 * g : 512 * g + 512].rearrange("p k (r t) -> p k t r", t=4)
+            if parts == 1:
+                eng.tensor_copy(out=u_s[:, h, g], in_=src)
+            else:
+                for k in range(2):
+                    w = 4 // (parts // 2)
+                    for t in range(0, 4, w):
+                        eng.tensor_copy(out=u_s[:, h, g, k, t : t + w], in_=src[:, k, t : t + w])
 
         def build_ee(h):
             for g in range(2):
@@ -301,27 +280,28 @@ def tile_approximate_inverse_gradient_s14_kernel(tc, m, u_words, u_scales, v_wor
                     done_q.add(cc)
                     quant_m(cc)
 
-        permute_codes(0, 0, 0)
-        permute_codes(0, 0, 1)
-        permute_scales(0, 0)
-        if CFG["p01"] == 1:
-            permute_codes(0, 1, 0)
-            permute_codes(0, 1, 1)
-            permute_scales(0, 1)
-        interleave(0)
-        done_i.add(0)
-        quant_m(0)
-        done_q.add(0)
-        if CFG["p01"] == 2:
-            interleave(1)
-            quant_m(1)
-            done_i.add(1)
-            done_q.add(1)
-        if CFG["p01"] != 1:
-            permute_codes(0, 1, 0)
-            permute_codes(0, 1, 1)
-            permute_scales(0, 1)
+        def permute(h, name, eng):
+            g = int(name[0])
+            parts = CFG["gp"] if eng is nc.gpsimd else 1
+            if name[1] == "s":
+                permute_scales(h, g, eng, parts)
+            else:
+                permute_codes(h, g, int(name[1]), eng, parts)
+
+        for name in CFG["g0"].split():
+            permute(0, name, nc.gpsimd)
+        for name in CFG["va"].split():
+            permute(0, name, nc.vector)
+        for cc in range(CFG["first"]):
+            interleave(cc)
+            quant_m(cc)
+            done_i.add(cc)
+            done_q.add(cc)
+        for name in CFG["vb"].split():
+            permute(0, name, nc.vector)
         build_ee(0)
+        for name in CFG["g1"].split():
+            permute(1, name, nc.gpsimd)
 
         def spread_step():
             pst = ps2p.tile([P, 1024], BF16, name="ps2")
@@ -355,12 +335,9 @@ def tile_approximate_inverse_gradient_s14_kernel(tc, m, u_words, u_scales, v_wor
                 build_ee(1)
             if n == CFG["spread"]:
                 spread_step()
-            for piece in range(6):
-                if CFG["perm"][piece] == n:
-                    if piece % 3 < 2:
-                        permute_codes(1, piece // 3, piece % 3)
-                    else:
-                        permute_scales(1, piece // 3)
+            for when, name in CFG["v1"]:
+                if when == n:
+                    permute(1, name, nc.vector)
             if 0 <= a < S:
                 unit, h, half, q, g = s1_parts(a)
                 b = q * RQ // 4

from contextlib import ExitStack

import concourse.mybir as mybir
from concourse.masks import make_identity

G, N = 2, 1024
FLOPS = 2 * 2 * G * N * N * N

F32 = mybir.dt.float32
BF16 = mybir.dt.bfloat16
U32 = mybir.dt.uint32
I32 = mybir.dt.int32
U8 = mybir.dt.uint8
FP8 = mybir.dt.float8_e4m3fn_x4
FP4 = mybir.dt.float4_e2m1fn_x4
ALU = mybir.AluOpType
AX = mybir.AxisListType
COPY = mybir.ActivationFunctionType.Copy

P = 128
CFG = {'lag': 2, 'gset': {0: (0, 2, 4), 1: (), 2: (), 3: ()}, 'vp': ((0, 1), (1, 1), (2, 1), (3, 1), (4, 1), (5, 1)), 'd1': 0, 'd2': 0, 'rq': 2, 'ee1': 4, 'spread': 4, 'halves': 2, 'ord0': ((0, 0), (1, 0), (0, 1), (1, 1), (2, 0), (3, 0), (2, 1), (3, 1)), 'ordn': ((0, 0), (0, 1), (1, 0), (1, 1), (2, 0), (2, 1), (3, 0), (3, 1)), 'ia': 3, 'qa': 3, 'sd': 3, 'loads': 'u00 mA us0 mB u01 sm mC mD u10 us1 v0 vs0 u11 n0 n1 vs1 v1', 'g0': '1s 11', 'va': '00 01 0s', 'vb': '10', 'g1': '00 01 10 11 1s', 'v1': ((9, '0s'),), 'first': 2, 'gp': 4}


def tile_approximate_inverse_gradient_s14_kernel(tc, m, u_words, u_scales, v_words, v_scales, e, step, out):
    nc = tc.nc
    with ExitStack() as ctx:
        keep = ctx.enter_context(tc.tile_pool(name="keep", bufs=1))
        mix = ctx.enter_context(tc.tile_pool(name="mix", bufs=4))
        rpool = ctx.enter_context(tc.tile_pool(name="rpool", bufs=2))
        opool = ctx.enter_context(tc.tile_pool(name="opool", bufs=8))
        tpool = ctx.enter_context(tc.tile_pool(name="tpool", bufs=3))
        ps1p = ctx.enter_context(tc.psum_pool(name="ps1p", bufs=4))
        ps2p = ctx.enter_context(tc.psum_pool(name="ps2p", bufs=4))
        ctx.enter_context(tc.manual_schedule())

        u_raw = keep.tile([P, G, 2, 2 * N], U8, name="u_raw", align_bytes=64)
        u_sraw = keep.tile([P, 2 * G, N], U8, name="u_sraw", align_bytes=64)
        u_w = keep.tile([P, G, 2, 2, 4, 256], U8, name="u_w", align_bytes=64)
        u_s = keep.tile([P, G, 2, 2, 4, 128], U8, name="u_s", align_bytes=64)
        v_raw = keep.tile([P, G, 2, 2 * N], U8, name="v_raw", align_bytes=64)
        v_s = keep.tile([P, 2 * G, N], U8, name="v_s", align_bytes=64)
        m_raw = [keep.tile([P, 2, 4, N], BF16, name="m_raw%d" % h, align_bytes=64) for h in range(G)]
        step_b = keep.tile([P, G * N], BF16, name="step_b", align_bytes=64)
        srow = keep.tile([P, P], BF16, name="srow", align_bytes=64)
        scol = keep.tile([P, 16], BF16, name="scol", align_bytes=64)
        e_raw = keep.tile([P, 2 * G, 4], BF16, name="e_raw", align_bytes=64)
        ident = keep.tile([P, P], BF16, name="ident", align_bytes=64)
        s4 = keep.tile([P, 32], F32, name="s4", align_bytes=64)
        qsel = keep.tile([P, 4], F32, name="qsel", align_bytes=64)
        ee = keep.tile([P, 2 * G, 128, 4], BF16, name="ee", align_bytes=64)

        u_raw_i = u_raw[:].bitcast(I32)
        v_raw_i = v_raw[:].bitcast(I32)
        u_sraw_i = u_sraw[:].bitcast(I32)
        v_s_i = v_s[:].bitcast(I32)
        uw_i = u_words.bitcast(I32)
        vw_i = v_words.bitcast(I32)
        us_i = u_scales.bitcast(I32)
        vs_i = v_scales.bitcast(I32)

        nc.vector.memset(u_sraw_i[:, 0:2], 0)
        nc.vector.memset(u_sraw_i[:, 2:4], 0)
        nc.vector.memset(v_s_i, 0)
        nc.gpsimd.memset(srow[:].bitcast(I32), 0)
        make_identity(nc, ident[:])
        nc.gpsimd.memset(ee[:].rearrange("p a b c -> p (a b c)").bitcast(I32), 0)

        def load_u(h, g):
            nc.sync.dma_start(
                out=u_raw_i[:, h, :, 256 * g : 256 * g + 256],
                in_=uw_i[2 * h : 2 * h + 2, :, 256 * g : 256 * g + 256].rearrange("k p n -> p k n"),
            )

        def load_m(h, k, c0, c1):
            nc.sync.dma_start(
                out=m_raw[h][:, k, :, c0:c1],
                in_=m[h, 512 * k : 512 * k + 512, c0:c1].rearrange("(p t) c -> p t c", t=4),
            )

        def load_scales(dst, src, a, b):
            for q in range(4):
                nc.sync.dma_start(
                    out=dst[32 * q : 32 * q + 4, a:b, :],
                    in_=src[a:b, 4 * q : 4 * q + 4, :].rearrange("k r n -> r k n"),
                )

        def load_small():
            nc.sync.dma_start(out=srow[0:16, :], in_=step.rearrange("h (a n) -> (h a) n", n=P))
            nc.sync.dma_start(out=e_raw[:], in_=e.rearrange("h (g p t) -> p (h g) t", g=2, t=4))

        def load_v(h):
            nc.sync.dma_start(out=v_raw_i[:, h], in_=vw_i[2 * h : 2 * h + 2].rearrange("k p n -> p k n"))

        def load_m2(h, a, b):
            load_m(h, 0, a, b)
            load_m(h, 1, a, b)

        loads = {
            "u00": lambda: load_u(0, 0), "u01": lambda: load_u(0, 1), "u10": lambda: load_u(1, 0), "u11": lambda: load_u(1, 1),
            "us0": lambda: load_scales(u_sraw_i, us_i, 0, 2), "us1": lambda: load_scales(u_sraw_i, us_i, 2, 4),
            "vs0": lambda: load_scales(v_s_i, vs_i, 0, 2), "vs1": lambda: load_scales(v_s_i, vs_i, 2, 4),
            "us": lambda: load_scales(u_sraw_i, us_i, 0, 4), "vs": lambda: load_scales(v_s_i, vs_i, 0, 4),
            "v0": lambda: load_v(0), "v1": lambda: load_v(1), "sm": load_small,
            "mA": lambda: load_m2(0, 0, 128), "mB": lambda: load_m2(0, 128, 256), "mAB": lambda: load_m2(0, 0, 256),
            "mC": lambda: load_m2(0, 256, 512), "mD": lambda: load_m2(0, 512, 1024), "mCD": lambda: load_m2(0, 256, 1024),
            "n0": lambda: load_m2(1, 0, 512), "n1": lambda: load_m2(1, 512, 1024), "n": lambda: load_m2(1, 0, 1024),
        }
        for token in CFG["loads"].split():
            loads[token]()

        nc.vector.tensor_reduce(out=s4[:], in_=ident[:].rearrange("p (q r) -> p r q", q=4), axis=AX.X, op=ALU.add)
        nc.vector.tensor_reduce(out=qsel[:], in_=ident[:].rearrange("p (q r) -> p q r", q=4), axis=AX.X, op=ALU.add)

        def permute_codes(h, g, k, eng, parts):
            dst = u_w[:, h, g, k].rearrange("p t (r b) -> p t r b", b=2)
            src = u_raw[:, h, k, 1024 * g : 1024 * g + 1024].rearrange("p (r t b) -> p t r b", t=4, b=2)
            w = 4 // parts
            for t in range(0, 4, w):
                eng.tensor_copy(out=dst[:, t : t + w], in_=src[:, t : t + w])

        def permute_scales(h, g, eng, parts):
            src = u_sraw[:, 2 * h : 2 * h + 2, 512 * g : 512 * g + 512].rearrange("p k (r t) -> p k t r", t=4)
            if parts == 1:
                eng.tensor_copy(out=u_s[:, h, g], in_=src)
            else:
                for k in range(2):
                    w = 4 // (parts // 2)
                    for t in range(0, 4, w):
                        eng.tensor_copy(out=u_s[:, h, g, k, t : t + w], in_=src[:, k, t : t + w])

        def build_ee(h):
            for g in range(2):
                hg = 2 * h + g
                nc.vector.tensor_tensor(
                    out=ee[:, hg].rearrange("p x t -> p (x t)").rearrange("p (r a) -> p r a", a=16)[:, :, 0:16:5],
                    in0=s4[:].unsqueeze(2).to_broadcast([P, 32, 4]),
                    in1=e_raw[:, hg].unsqueeze(1).to_broadcast([P, 32, 4]),
                    op=ALU.mult,
                )

        mi = {}
        mq = {}

        def interleave(cc):
            h, c0 = cc // 8, 128 * (cc % 8)
            t = mix.tile([P, 2, 128, 4], BF16, name="mi", align_bytes=64)
            mi[cc] = t
            src = m_raw[h][:, :, :, c0 : c0 + 128]
            for k in range(2):
                if (cc, k) in CFG["vp"]:
                    nc.vector.tensor_copy(out=t[:, k], in_=src[:, k].rearrange("p t c -> p c t"))
            if (cc, 1) in CFG["vp"]:
                if (cc, 0) not in CFG["vp"]:
                    nc.scalar.copy(out=t[:, 0], in_=src[:, 0].rearrange("p t c -> p c t"))
            else:
                nc.scalar.copy(out=t[:], in_=src.rearrange("p k t c -> p k c t"))

        def quant_m(cc):
            codes = mix.tile([P, 256], U32, name="mcodes", align_bytes=64)
            scales = mix.tile([P, 256], U8, name="mscales", align_bytes=64)
            mq[cc] = (codes, scales)
            nc.vector.quantize_mx(
                out=codes[:].bitcast(FP8), scales=scales[:], in_=mi[cc][:].rearrange("p k c t -> p (k c t)")
            )

        order1 = []
        for unit in range(4):
            for q, d in CFG["ordn"] if unit else CFG["ord0"]:
                order1.append((unit, q, d))
        first_use = {}
        for i in range(32):
            first_use.setdefault(4 * order1[i][0] + order1[i][1], i)

        units = {}
        ps1 = {}
        ps2 = {}

        def s1_parts(n):
            unit, q, d = order1[n]
            h, half = unit // 2, unit % 2
            g = half if d == 0 else 1 - half
            if unit == 0:
                g = d
            return unit, h, half, q, g

        def s1_mm(n):
            unit, h, half, q, g = s1_parts(n)
            codes, scales = mq[4 * order1[n][0] + order1[n][1]]
            ps = ps1p.tile([P, 4, 128], F32, name="ps1")
            ps1[n] = ps
            for t in range(4):
                for k in range(2):
                    nc.tensor.matmul_mx(
                        out=ps[:, t, :],
                        lhsT=u_w[:, h, g, k, t, :].bitcast(FP4),
                        lhsT_scale=u_s[:, h, g, k, t, :],
                        rhs=codes[:, 128 * k : 128 * k + 128].bitcast(FP8),
                        rhs_scale=scales[:, 128 * k : 128 * k + 128],
                        start=(k == 0),
                        stop=(k == 1),
                    )

        def s1_evac(n):
            unit, h, half, q, g = s1_parts(n)
            if n % 8 == 0:
                units[unit] = (
                    rpool.tile([P, 2, 512, 4], BF16, name="rb", align_bytes=64),
                    rpool.tile([P, 2, 512], U32, name="rcodes", align_bytes=64),
                    rpool.tile([P, 2, 512], U8, name="rscales", align_bytes=64),
                )
            rb = units[unit][0]
            dst = rb[:, g, 128 * q : 128 * q + 128, :]
            src = ps1[n][:].rearrange("p t c -> p c t")
            if g == half:
                nc.vector.scalar_tensor_tensor(
                    out=dst, in0=ee[:, 2 * h + g], scalar=qsel[:, q : q + 1], in1=src, op0=ALU.mult, op1=ALU.subtract
                )
            else:
                nc.scalar.activation(out=dst, in_=src, func=COPY, scale=-1.0)

        def quant_r(unit, g, b):
            rb, rc, rs = units[unit]
            if True:
                w = 512 // CFG["rq"]
                cols = slice(w * b, w * b + w)
                nc.vector.quantize_mx(
                    out=rc[:, g, cols].bitcast(FP8),
                    scales=rs[:, g, cols],
                    in_=rb[:, g, cols, :].rearrange("p c t -> p (c t)"),
                )

        def s2_mm(n):
            unit, j = n // 8, n % 8
            h = unit // 2
            rb, rc, rs = units[unit]
            ps = ps2p.tile([P, 512], F32, name="ps2")
            ps2[n] = ps
            for g in range(2):
                nc.tensor.matmul_mx(
                    out=ps[:],
                    lhsT=v_raw[:, h, g, 256 * j : 256 * j + 256].bitcast(FP4),
                    lhsT_scale=v_s[:, 2 * h + g, 128 * j : 128 * j + 128],
                    rhs=rc[:, g, :].bitcast(FP8),
                    rhs_scale=rs[:, g, :],
                    start=(g == 0),
                    stop=(g == 1),
                )

        def s2_evac(n):
            unit, j = n // 8, n % 8
            h, c0 = unit // 2, 512 * (unit % 2)
            ot = opool.tile([P, 512], F32, name="ot", align_bytes=64)
            st = step_b[:, N * h + c0 : N * h + c0 + 512]
            if j in CFG["gset"][unit]:
                tmp = tpool.tile([P, 512], F32, name="tmp", align_bytes=64)
                nc.scalar.copy(out=tmp[:], in_=ps2[n][:])
                w = 512 // CFG["halves"]
                for a in range(0, 512, w):
                    nc.gpsimd.tensor_tensor(out=ot[:, a : a + w], in0=tmp[:, a : a + w], in1=st[:, a : a + w], op=ALU.mult)
            else:
                nc.vector.tensor_tensor(out=ot[:], in0=ps2[n][:], in1=st, op=ALU.mult)
            stores.append((n + (CFG["sd"] if j in CFG["gset"][unit] else 0), out[h, 128 * j : 128 * j + 128, c0 : c0 + 512], ot))

        stores = []

        def flush(n):
            for item in list(stores):
                if item[0] <= n:
                    nc.sync.dma_start(out=item[1], in_=item[2][:])
                    stores.remove(item)

        done_i, done_q = set(), set()

        def prepare(n):
            for cc in range(16):
                if first_use[cc] <= n + CFG["ia"] and cc not in done_i:
                    done_i.add(cc)
                    interleave(cc)
                if first_use[cc] <= n + CFG["qa"] and cc not in done_q:
                    done_q.add(cc)
                    quant_m(cc)

        def permute(h, name, eng):
            g = int(name[0])
            parts = CFG["gp"] if eng is nc.gpsimd else 1
            if name[1] == "s":
                permute_scales(h, g, eng, parts)
            else:
                permute_codes(h, g, int(name[1]), eng, parts)

        for name in CFG["g0"].split():
            permute(0, name, nc.gpsimd)
        for name in CFG["va"].split():
            permute(0, name, nc.vector)
        for cc in range(CFG["first"]):
            interleave(cc)
            quant_m(cc)
            done_i.add(cc)
            done_q.add(cc)
        for name in CFG["vb"].split():
            permute(0, name, nc.vector)
        build_ee(0)
        for name in CFG["g1"].split():
            permute(1, name, nc.gpsimd)

        def spread_step():
            pst = ps2p.tile([P, 1024], BF16, name="ps2")
            nc.tensor.transpose(pst[:, 0:P], srow[:], ident[:])
            nc.scalar.copy(out=scol[:], in_=pst[:, 0:16])
            for h in range(G):
                psb = ps2p.tile([P, 1024], BF16, name="ps2")
                for a in range(8):
                    nc.tensor.transpose(
                        psb[:, P * a : P * a + P], scol[:, 8 * h + a : 8 * h + a + 1].to_broadcast([P, P]), ident[:]
                    )
                nc.scalar.copy(out=step_b[:, N * h : N * h + N], in_=psb[:])

        S = 32
        LAG, D1, D2, RQ = CFG["lag"], CFG["d1"], CFG["d2"], CFG["rq"]
        seen = {}
        for n in range(S + 8 + LAG + 2):
            prepare(n)
            if n < S:
                s1_mm(n)
            k = n - 8 - LAG
            if 0 <= k < S:
                s2_mm(k)
            a = n - D1
            if 0 <= a < S:
                s1_evac(a)
            if 0 <= k - D2 < S:
                s2_evac(k - D2)
            flush(k - D2)
            if n == CFG["ee1"]:
                build_ee(1)
            if n == CFG["spread"]:
                spread_step()
            for when, name in CFG["v1"]:
                if when == n:
                    permute(1, name, nc.vector)
            if 0 <= a < S:
                unit, h, half, q, g = s1_parts(a)
                b = q * RQ // 4
                seen[(unit, g, b)] = seen.get((unit, g, b), 0) + 1
                if seen[(unit, g, b)] == 4 // RQ:
                    quant_r(unit, g, b)
        flush(S + 10)
